import numpy as np
import ml_dtypes


def mxq(x, axis, fmt="e4m3"):
    dtype, down = {"e4m3": (ml_dtypes.float8_e4m3fn, 7), "e5m2": (ml_dtypes.float8_e5m2, 14)}[fmt]
    v = np.moveaxis(np.asarray(x, np.float32).astype(ml_dtypes.bfloat16).astype(np.float64), axis, -1)
    blocks = v.reshape(v.shape[:-1] + (-1, 32))
    amax = np.abs(blocks).max(-1, keepdims=True)
    byte = np.maximum(np.where(amax > 0, np.frexp(amax)[1] - 1 + 127, 0) - down, 1)
    scale = np.exp2(byte - 127.0)
    codes = (blocks / scale).astype(np.float32).astype(dtype).astype(np.float64)
    return np.moveaxis((codes * scale).reshape(v.shape), -1, axis)


WIDE = False


def mx_kscale(k):
    if not WIDE:
        return np.ones(k)
    levels = np.array([10, -10, 5, -5, 0])
    if k % 512:
        return np.exp2(np.random.permutation(np.resize(levels, k // 32))).repeat(32)
    a = np.empty((k // 512, 16))
    for p in range(k // 512):
        a[p, :8] = np.random.permutation(np.resize(levels, 8))
        for g in range(8):
            far = levels[np.abs(levels - a[p, g]) >= 10]
            a[p, g + 8] = far[np.random.randint(len(far))]
    return np.exp2(a.ravel()).repeat(32)


def f64(x):
    return np.asarray(x).astype(np.float64)


def striped(idx):
    return np.tile(idx.reshape(-1, 16).T, (8, 1)).astype(np.uint16)


def unstriped(offs):
    return offs[:16].T.reshape(-1).astype(np.int64)


E2M1 = np.array([0.0, 0.5, 1.0, 1.5, 2.0, 3.0, 4.0, 6.0, -0.0, -0.5, -1.0, -1.5, -2.0, -3.0, -4.0, -6.0])


def pack_weight(w, fmt):
    k, n = w.shape
    w = f64(np.asarray(w, np.float32).astype(ml_dtypes.bfloat16)).reshape(k // 32, 32, n)
    amax = np.abs(w).max(1)
    if fmt == "e4m3":
        byte = np.frexp(amax)[1] - 1 + 127 - 7
    else:
        mant, ex = np.frexp(amax / 6.0)
        byte = np.where(mant > 0.5, ex, ex - 1) + 127
    byte = np.clip(np.where(amax > 0, byte, 1), 1, 254)
    scaled = (w * np.exp2(127.0 - byte)[:, None, :]).reshape(k, n).astype(np.float32)
    by_word = np.ascontiguousarray(scaled.reshape(k // 512, 128, 4, n).transpose(0, 1, 3, 2))
    if fmt == "e4m3":
        words = by_word.astype(ml_dtypes.float8_e4m3fn).view(np.uint8)
    else:
        c = by_word.astype(ml_dtypes.float4_e2m1fn).view(np.uint8) & 0xF
        words = (c[..., 0::2] | (c[..., 1::2] << 4)).reshape(k // 512, 128, 2 * n)
    return np.ascontiguousarray(words), np.ascontiguousarray(byte.astype(np.uint8).reshape(k // 512, 16, n))


def unpack_weight(words, scales, fmt):
    g, _, n = scales.shape
    words = np.ascontiguousarray(words).reshape(g, 128, n, -1)
    if fmt == "e4m3":
        vals = words.view(ml_dtypes.float8_e4m3fn).astype(np.float64)
    else:
        nib = np.empty((g, 128, n, 4), np.uint8)
        nib[..., 0::2] = words & 0xF
        nib[..., 1::2] = words >> 4
        vals = E2M1[nib]
    vals = vals * np.repeat(np.exp2(scales.astype(np.float64) - 127.0), 8, axis=1)[..., None]
    return vals.transpose(0, 1, 3, 2).reshape(g * 512, n)


def gelu(v):
    return 0.5 * v * (1.0 + np.tanh(np.sqrt(2.0 / np.pi) * (v + 0.044715 * v**3)))


K, T, S, H, T3, S2 = 1024, 2048, 512, 512, 2048, 512

def setup_inputs():
    n = np.random.standard_normal
    s = mx_kscale(K)[:, None]
    u = mx_kscale(H)[:, None]
    tab_words, tab_scales = pack_weight(n((K, T)) * s, "e4m3")
    tab2_words, tab2_scales = pack_weight(n((H, T3)) / np.sqrt(H) / u, "e4m3")
    tab3_words, tab3_scales = pack_weight(n((H, T3)) / np.sqrt(H) / u, "e4m3")
    w1_words, w1_scales = pack_weight(1.3 * n((K, H)) / np.sqrt(K) / s, "e2m1")
    w3_words, w3_scales = pack_weight(0.3 * n((K, H)) / np.sqrt(K) / s, "e4m3")
    return {
        "tab_words": tab_words, "tab_scales": tab_scales,
        "tab2_words": tab2_words, "tab2_scales": tab2_scales,
        "tab3_words": tab3_words, "tab3_scales": tab3_scales,
        "offs": striped(np.random.permutation(T)[:S]),
        "offs2": striped(np.random.permutation(T3)[:S2]),
        "offs3": striped(np.random.permutation(T3)[:S2]),
        "w1_words": w1_words, "w1_scales": w1_scales,
        "w2": (0.54 * n((K, H)) / np.sqrt(K) / s).astype(np.float32),
        "w3_words": w3_words, "w3_scales": w3_scales,
        "gain": (2.0 * np.exp(0.3 * n(H)) * u[:, 0]).astype(np.float32),
        "d": (0.5 * n(S2)).astype(np.float32),
    }

def reference(tab_words, tab_scales, tab2_words, tab2_scales, tab3_words, tab3_scales, offs, offs2, offs3,
              w1_words, w1_scales, w2, w3_words, w3_scales, gain, d):
    v = unpack_weight(tab_words, tab_scales, "e4m3")[:, unstriped(offs)]
    v2 = unpack_weight(tab2_words, tab2_scales, "e4m3")[:, unstriped(offs2)]
    v3 = unpack_weight(tab3_words, tab3_scales, "e4m3")[:, unstriped(offs3)]
    w1 = unpack_weight(w1_words, w1_scales, "e2m1")
    w3 = unpack_weight(w3_words, w3_scales, "e4m3")
    taste = w1.T @ v
    pace = mxq(f64(w2), 0, "e4m3").T @ v
    plain = w3.T @ v
    h = (np.tanh(taste) * np.sin(pace) + plain) * f64(gain)[:, None]
    hq = mxq(h, 0, "e4m3")
    e2 = v2.T @ hq
    e3 = v3.T @ hq
    return np.minimum(e2, e3) + f64(d)[:, None]

@@ -1,0 +1,252 @@
+from contextlib import ExitStack
+
+import concourse.mybir as mybir
+from concourse.masks import make_identity
+
+K, T, S, H, S2 = 1024, 2048, 512, 512, 512
+FLOPS = 2 * (3 * K * H * S + 2 * H * S2 * S)
+
+F32 = mybir.dt.float32
+BF16 = mybir.dt.bfloat16
+I32 = mybir.dt.int32
+U32 = mybir.dt.uint32
+U16 = mybir.dt.uint16
+U8 = mybir.dt.uint8
+FP8X4 = mybir.dt.float8_e4m3fn_x4
+FP4X4 = mybir.dt.float4_e2m1fn_x4
+ACT = mybir.ActivationFunctionType
+ALU = mybir.AluOpType
+
+P = 128
+PACK = 4
+PASSES = K // (P * PACK)
+HALF = 256
+ROW_V2, ROW_V3, ROW_W3 = 4, 8, 12
+
+
+def tile_list_hiker_date_scores_kernel(tc, tab_words, tab_scales, tab2_words, tab2_scales, tab3_words,
+                                                 tab3_scales, offs, offs2, offs3, w1_words, w1_scales, w2,
+                                                 w3_words, w3_scales, gain, d, out):
+    nc = tc.nc
+    with ExitStack() as ctx:
+        keep = ctx.enter_context(tc.tile_pool(name="keep", bufs=1))
+        work = ctx.enter_context(tc.tile_pool(name="work", bufs=4))
+        psum = ctx.enter_context(tc.psum_pool(name="psum", bufs=1))
+
+        def kept(shape, dtype, name):
+            return keep.tile(shape, dtype, name=name, align_bytes=64)
+
+        def zero(engine, plane):
+            engine.memset(plane[:].rearrange("p a t -> p (a t)").bitcast(I32), 0)
+
+        def load_scales(engine, plane, scales, row):
+            for q in range(4):
+                engine.dma_start(
+                    out=plane[32 * q + row : 32 * q + row + 4].bitcast(I32),
+                    in_=scales[:, 4 * q : 4 * q + 4, :].rearrange("a r t -> r a t").bitcast(I32),
+                )
+
+        def load_words(tile, words):
+            nc.sync.dma_start(out=tile[:].bitcast(I32), in_=words.rearrange("p t i -> p (t i)").bitcast(I32))
+
+        idx1 = kept([P, S // 16], U16, "idx1")
+        idx2 = kept([P, S2 // 16], U16, "idx2")
+        idx3 = kept([P, S2 // 16], U16, "idx3")
+        tab_plane = kept([P, PASSES, T], U8, "tab_plane")
+        tab2_plane = kept([P, 1, T], U8, "tab2_plane")
+        tab3_plane = kept([P, 1, T], U8, "tab3_plane")
+        w1_plane = kept([P, PASSES, H], U8, "w1_plane")
+        w3_plane = kept([P, PASSES, H], U8, "w3_plane")
+        tab = [kept([P, T], U32, "tab%d" % a) for a in range(PASSES)]
+        tab2 = kept([P, T], U32, "tab2")
+        tab3 = kept([P, T], U32, "tab3")
+        w2_raw = [kept([P, PACK, H], F32, "w2_raw%d" % a) for a in range(PASSES)]
+        w1 = kept([P, PASSES, 2 * H], U8, "w1")
+        w3 = kept([P, PASSES, H], U32, "w3")
+        gain_sb = kept([P, PACK], F32, "gain_sb")
+        d_sb = kept([P, S2 // P], F32, "d_sb")
+        ident = kept([P, P], F32, "ident")
+
+        for plane in (tab_plane, tab3_plane, w1_plane, w3_plane, tab2_plane):
+            zero(nc.vector, plane)
+
+        def load_w2(a):
+            nc.sync.dma_start(out=w2_raw[a][:], in_=w2[512 * a : 512 * (a + 1), :].rearrange("(p i) c -> p i c", i=PACK))
+
+        nc.sync.dma_start(out=idx1[:], in_=offs)
+        load_w2(0)
+        load_scales(nc.sync, tab_plane, tab_scales, 0)
+        load_words(tab[0], tab_words[0])
+        load_w2(1)
+        nc.sync.dma_start(out=idx2[:], in_=offs2)
+        load_scales(nc.sync, w1_plane, w1_scales, 0)
+        nc.sync.dma_start(out=w1[:].bitcast(I32), in_=w1_words.rearrange("a p c -> p a c").bitcast(I32))
+        load_words(tab[1], tab_words[1])
+        nc.sync.dma_start(out=idx3[:], in_=offs3)
+        load_scales(nc.sync, tab2_plane, tab2_scales, ROW_V2)
+        nc.sync.dma_start(out=w3[:].bitcast(I32), in_=w3_words.rearrange("a p c i -> p a (c i)").bitcast(I32))
+        load_words(tab2, tab2_words[0])
+        load_words(tab3, tab3_words[0])
+        nc.gpsimd.dma_start(out=gain_sb[:], in_=gain.rearrange("(p t) -> p t", t=PACK))
+        load_scales(nc.gpsimd, tab3_plane, tab3_scales, ROW_V3)
+        load_scales(nc.gpsimd, w3_plane, w3_scales, ROW_W3)
+        make_identity(nc, ident[:])
+        with nc.allow_non_contiguous_dma(reason="one value of d for each partition and tile of candidates"):
+            nc.gpsimd.dma_start(out=d_sb[:], in_=d.rearrange("(c p) -> p c", p=P))
+
+        v = [kept([P, S], U32, "v%d" % a) for a in range(PASSES)]
+        v_sc = [kept([P, S], U8, "v_sc%d" % a) for a in range(PASSES)]
+        v2 = kept([P, S2], U32, "v2")
+        v3 = kept([P, S2], U32, "v3")
+        v2_sc = kept([P, S2], U8, "v2_sc")
+        v3_sc = kept([P, S2], U8, "v3_sc")
+        w2_bf = [[kept([P, HALF, PACK], BF16, "w2_bf%d%d" % (a, u)) for u in range(2)] for a in range(PASSES)]
+        w2_codes = [kept([P, H], U32, "w2_codes%d" % a) for a in range(PASSES)]
+        w2_sc = [kept([P, H], U8, "w2_sc%d" % a) for a in range(PASSES)]
+        h_bf = [kept([P, HALF, PACK], BF16, "h_bf%d" % u) for u in range(2)]
+        h_codes = [kept([P, HALF], U32, "h_codes%d" % u) for u in range(2)]
+        h_sc = [kept([P, HALF], U8, "h_sc%d" % u) for u in range(2)]
+
+        def gather(dst, window, idx):
+            nc.vector.tensor_copy(out=dst, in_=window.indirect(idx))
+
+        def round_w2(copy, a, u):
+            copy(
+                out=w2_bf[a][u][:].rearrange("p (c e) i -> p c i e", e=4),
+                in_=w2_raw[a][:, :, HALF * u : HALF * (u + 1)].rearrange("p i (c e) -> p c i e", e=4),
+            )
+
+        def quantize(codes, scales, grouped):
+            nc.vector.quantize_mx(out=codes.bitcast(FP8X4), scales=scales, in_=grouped[:].rearrange("p c i -> p (c i)"))
+
+        def quantize_w2(a, u):
+            cols = slice(HALF * u, HALF * (u + 1))
+            quantize(w2_codes[a][:, cols], w2_sc[a][:, cols], w2_bf[a][u])
+
+        round_w2(nc.scalar.copy, 0, 0)
+        round_w2(nc.scalar.copy, 0, 1)
+        gather(v_sc[0][:], tab_plane[:, 0, :], idx1[:])
+        gather(v_sc[1][:], tab_plane[:, 1, :], idx1[:])
+        gather(v[0][:], tab[0][:], idx1[:])
+        quantize_w2(0, 0)
+        quantize_w2(0, 1)
+        round_w2(nc.scalar.copy, 1, 0)
+        round_w2(nc.vector.tensor_copy, 1, 1)
+        gather(v3_sc[:], tab3_plane[:, 0, :], idx3[:])
+        quantize_w2(1, 1)
+        quantize_w2(1, 0)
+        for u in range(2):
+            gather(v[1][:, HALF * u : HALF * (u + 1)], tab[1][:], idx1[:, 16 * u : 16 * (u + 1)])
+        gather(v2_sc[:], tab2_plane[:, 0, :], idx2[:])
+
+        weights = {
+            "taste": lambda a: (w1[:, a, :].bitcast(FP4X4), w1_plane[:, a, :]),
+            "pace": lambda a: (w2_codes[a][:].bitcast(FP8X4), w2_sc[a][:]),
+            "plain": lambda a: (w3[:, a, :].bitcast(FP8X4), w3_plane[ROW_W3:, a, :]),
+        }
+        banks = {}
+        vals = {}
+
+        def new_bank():
+            return psum.tile([P, 512], F32, name="bank", tag="bank", bufs=6)
+
+        def first_pass(kind, jt, a):
+            if a == 0:
+                banks[kind, jt] = new_bank()
+            cols = slice(P * jt, P * (jt + 1))
+            codes, scales = weights[kind](a)
+            nc.tensor.matmul_mx(out=banks[kind, jt][:], lhsT=v[a][:, cols].bitcast(FP8X4), lhsT_scale=v_sc[a][:, cols],
+                                rhs=codes, rhs_scale=scales, start=(a == 0), stop=(a == PASSES - 1))
+
+        def leave(kind, jt):
+            vals[kind, jt] = work.tile([P, PACK, P], F32, name=kind)
+            src = banks[kind, jt][:].rearrange("p (m t) -> p t m", t=PACK)
+            if kind == "plain":
+                nc.scalar.copy(out=vals[kind, jt][:], in_=src)
+            else:
+                nc.scalar.activation(out=vals[kind, jt][:], in_=src, func=ACT.Tanh if kind == "taste" else ACT.Sin)
+
+        def product(jt):
+            vals["prod", jt] = work.tile([P, PACK, P], F32, name="prod")
+            nc.vector.tensor_tensor(out=vals["prod", jt][:], in0=vals["taste", jt][:], in1=vals["pace", jt][:], op=ALU.mult)
+
+        def turn(jt):
+            turned = psum.tile([P, PACK, P], F32, name="turned", tag="turned", bufs=2)
+            for t in range(PACK):
+                nc.tensor.matmul(out=turned[:, t, :], lhsT=vals["plain", jt][:, t, :], rhs=ident[:],
+                                 is_transpose=True, start=True, stop=False)
+                nc.tensor.matmul(out=turned[:, t, :], lhsT=vals["prod", jt][:, t, :], rhs=ident[:],
+                                 is_transpose=True, start=False, stop=True)
+            u, c = divmod(jt, 2)
+            nc.vector.tensor_tensor(
+                out=h_bf[u][:, P * c : P * (c + 1), :],
+                in0=turned[:].rearrange("p t j -> p j t"),
+                in1=gain_sb[:].unsqueeze(1).to_broadcast([P, P, PACK]),
+                op=ALU.mult,
+            )
+
+        def scores(codes, scales, row, u, pair):
+            bank = new_bank()
+            for c in range(2):
+                cols = slice(P * (2 * pair + c), P * (2 * pair + c + 1))
+                nc.tensor.matmul_mx(out=bank[:, HALF * c : HALF * (c + 1)], lhsT=codes[:, cols].bitcast(FP8X4),
+                                    lhsT_scale=scales[row:, cols], rhs=h_codes[u][:].bitcast(FP8X4),
+                                    rhs_scale=h_sc[u][:], start=True, stop=True)
+            return bank
+
+        def partners(u):
+            for pair in range(2):
+                bank = scores(v2, v2_sc, ROW_V2, u, pair)
+                for c in range(2):
+                    mt = 2 * pair + c
+                    vals["e2", u, mt] = work.tile([P, HALF], F32, name="e2", bufs=8)
+                    nc.scalar.activation(out=vals["e2", u, mt][:], in_=bank[:, HALF * c : HALF * (c + 1)],
+                                         func=ACT.Identity, bias=d_sb[:, mt : mt + 1])
+
+        def trails(u):
+            for pair in range(2):
+                bank = scores(v3, v3_sc, ROW_V3, u, pair)
+                for c in range(2):
+                    mt = 2 * pair + c
+                    result = work.tile([P, HALF], F32, name="result", bufs=8)
+                    nc.vector.scalar_tensor_tensor(out=result[:], in0=bank[:, HALF * c : HALF * (c + 1)],
+                                                   scalar=d_sb[:, mt : mt + 1], in1=vals["e2", u, mt][:],
+                                                   op0=ALU.add, op1=ALU.min)
+                    nc.sync.dma_start(out=out[P * mt : P * (mt + 1), HALF * u : HALF * (u + 1)], in_=result[:])
+
+        def whole(kind, jt):
+            first_pass(kind, jt, 0)
+            first_pass(kind, jt, 1)
+            leave(kind, jt)
+
+        for jt in range(4):
+            first_pass("taste", jt, 0)
+        for jt in range(2):
+            first_pass("pace", jt, 0)
+        for jt in range(4):
+            first_pass("taste", jt, 1)
+            leave("taste", jt)
+        for jt in range(2):
+            first_pass("pace", jt, 1)
+            leave("pace", jt)
+            product(jt)
+        whole("plain", 0)
+        whole("pace", 2)
+        gather(v2[:], tab2[:], idx2[:])
+        turn(0)
+        product(2)
+        whole("plain", 1)
+        whole("pace", 3)
+        turn(1)
+        product(3)
+        whole("plain", 2)
+        quantize(h_codes[0][:], h_sc[0][:], h_bf[0])
+        whole("plain", 3)
+        turn(2)
+        gather(v3[:], tab3[:], idx3[:])
+        partners(0)
+        turn(3)
+        trails(0)
+        quantize(h_codes[1][:], h_sc[1][:], h_bf[1])
+        partners(1)
+        trails(1)

@@ -33,8 +33,8 @@ def tile_list_hiker_date_scores_kernel(tc, tab_words, tab_scales, tab2_words, ta
         work = ctx.enter_context(tc.tile_pool(name="work", bufs=4))
         psum = ctx.enter_context(tc.psum_pool(name="psum", bufs=1))
 
-        def kept(shape, dtype, name):
-            return keep.tile(shape, dtype, name=name, align_bytes=64)
+        def kept(shape, dtype, name, tag=None):
+            return keep.tile(shape, dtype, name=name, tag=tag or name, align_bytes=64)
 
         def zero(engine, plane):
             engine.memset(plane[:].rearrange("p a t -> p (a t)").bitcast(I32), 0)
@@ -67,30 +67,30 @@ def tile_list_hiker_date_scores_kernel(tc, tab_words, tab_scales, tab2_words, ta
         d_sb = kept([P, S2 // P], F32, "d_sb")
         ident = kept([P, P], F32, "ident")
 
-        for plane in (tab_plane, tab3_plane, w1_plane, w3_plane, tab2_plane):
+        for plane in (tab3_plane, tab_plane, tab2_plane, w1_plane, w3_plane):
             zero(nc.vector, plane)
 
         def load_w2(a):
             nc.sync.dma_start(out=w2_raw[a][:], in_=w2[512 * a : 512 * (a + 1), :].rearrange("(p i) c -> p i c", i=PACK))
 
         nc.sync.dma_start(out=idx1[:], in_=offs)
-        load_w2(0)
-        load_scales(nc.sync, tab_plane, tab_scales, 0)
-        load_words(tab[0], tab_words[0])
-        load_w2(1)
         nc.sync.dma_start(out=idx2[:], in_=offs2)
-        load_scales(nc.sync, w1_plane, w1_scales, 0)
-        nc.sync.dma_start(out=w1[:].bitcast(I32), in_=w1_words.rearrange("a p c -> p a c").bitcast(I32))
-        load_words(tab[1], tab_words[1])
         nc.sync.dma_start(out=idx3[:], in_=offs3)
-        load_scales(nc.sync, tab2_plane, tab2_scales, ROW_V2)
+        load_words(tab[0], tab_words[0])
+        load_scales(nc.sync, tab_plane, tab_scales, 0)
+        load_words(tab[1], tab_words[1])
+        nc.sync.dma_start(out=w1[:].bitcast(I32), in_=w1_words.rearrange("a p c -> p a c").bitcast(I32))
+        load_scales(nc.sync, w1_plane, w1_scales, 0)
+        load_w2(0)
+        load_scales(nc.sync, w3_plane, w3_scales, ROW_W3)
+        load_w2(1)
         nc.sync.dma_start(out=w3[:].bitcast(I32), in_=w3_words.rearrange("a p c i -> p a (c i)").bitcast(I32))
         load_words(tab2, tab2_words[0])
         load_words(tab3, tab3_words[0])
-        nc.gpsimd.dma_start(out=gain_sb[:], in_=gain.rearrange("(p t) -> p t", t=PACK))
-        load_scales(nc.gpsimd, tab3_plane, tab3_scales, ROW_V3)
-        load_scales(nc.gpsimd, w3_plane, w3_scales, ROW_W3)
         make_identity(nc, ident[:])
+        load_scales(nc.gpsimd, tab3_plane, tab3_scales, ROW_V3)
+        load_scales(nc.gpsimd, tab2_plane, tab2_scales, ROW_V2)
+        nc.gpsimd.dma_start(out=gain_sb[:], in_=gain.rearrange("(p t) -> p t", t=PACK))
         with nc.allow_non_contiguous_dma(reason="one value of d for each partition and tile of candidates"):
             nc.gpsimd.dma_start(out=d_sb[:], in_=d.rearrange("(c p) -> p c", p=P))
 
@@ -98,8 +98,6 @@ def tile_list_hiker_date_scores_kernel(tc, tab_words, tab_scales, tab2_words, ta
         v_sc = [kept([P, S], U8, "v_sc%d" % a) for a in range(PASSES)]
         v2 = kept([P, S2], U32, "v2")
         v3 = kept([P, S2], U32, "v3")
-        v2_sc = kept([P, S2], U8, "v2_sc")
-        v3_sc = kept([P, S2], U8, "v3_sc")
         w2_bf = [[kept([P, HALF, PACK], BF16, "w2_bf%d%d" % (a, u)) for u in range(2)] for a in range(PASSES)]
         w2_codes = [kept([P, H], U32, "w2_codes%d" % a) for a in range(PASSES)]
         w2_sc = [kept([P, H], U8, "w2_sc%d" % a) for a in range(PASSES)]
@@ -123,20 +121,18 @@ def tile_list_hiker_date_scores_kernel(tc, tab_words, tab_scales, tab2_words, ta
             cols = slice(HALF * u, HALF * (u + 1))
             quantize(w2_codes[a][:, cols], w2_sc[a][:, cols], w2_bf[a][u])
 
-        round_w2(nc.scalar.copy, 0, 0)
-        round_w2(nc.scalar.copy, 0, 1)
         gather(v_sc[0][:], tab_plane[:, 0, :], idx1[:])
-        gather(v_sc[1][:], tab_plane[:, 1, :], idx1[:])
         gather(v[0][:], tab[0][:], idx1[:])
-        quantize_w2(0, 0)
-        quantize_w2(0, 1)
-        round_w2(nc.scalar.copy, 1, 0)
-        round_w2(nc.vector.tensor_copy, 1, 1)
+        gather(v_sc[1][:], tab_plane[:, 1, :], idx1[:])
+        gather(v[1][:], tab[1][:], idx1[:])
+        v3_sc = kept([P, S2], U8, "v3_sc", tag="tab1")
         gather(v3_sc[:], tab3_plane[:, 0, :], idx3[:])
-        quantize_w2(1, 1)
-        quantize_w2(1, 0)
-        for u in range(2):
-            gather(v[1][:, HALF * u : HALF * (u + 1)], tab[1][:], idx1[:, 16 * u : 16 * (u + 1)])
+        for a in range(PASSES):
+            for u in range(2):
+                round_w2(nc.vector.tensor_copy, a, u)
+            for u in range(2):
+                quantize_w2(a, u)
+        v2_sc = kept([P, S2], U8, "v2_sc", tag="w2_raw1")
         gather(v2_sc[:], tab2_plane[:, 0, :], idx2[:])
 
         weights = {
@@ -220,33 +216,26 @@ def tile_list_hiker_date_scores_kernel(tc, tab_words, tab_scales, tab2_words, ta
             leave(kind, jt)
 
         for jt in range(4):
-            first_pass("taste", jt, 0)
-        for jt in range(2):
+            whole("taste", jt)
+        for jt in range(4):
             first_pass("pace", jt, 0)
         for jt in range(4):
-            first_pass("taste", jt, 1)
-            leave("taste", jt)
-        for jt in range(2):
             first_pass("pace", jt, 1)
             leave("pace", jt)
-            product(jt)
-        whole("plain", 0)
-        whole("pace", 2)
+            whole("plain", jt)
         gather(v2[:], tab2[:], idx2[:])
+        product(0)
+        product(1)
         turn(0)
         product(2)
-        whole("plain", 1)
-        whole("pace", 3)
         turn(1)
-        product(3)
-        whole("plain", 2)
-        quantize(h_codes[0][:], h_sc[0][:], h_bf[0])
-        whole("plain", 3)
-        turn(2)
         gather(v3[:], tab3[:], idx3[:])
+        quantize(h_codes[0][:], h_sc[0][:], h_bf[0])
+        product(3)
+        turn(2)
         partners(0)
-        turn(3)
         trails(0)
+        turn(3)
         quantize(h_codes[1][:], h_sc[1][:], h_bf[1])
         partners(1)
         trails(1)

@@ -60,35 +60,39 @@ def tile_list_hiker_date_scores_kernel(tc, tab_words, tab_scales, tab2_words, ta
         tab = [kept([P, T], U32, "tab%d" % a) for a in range(PASSES)]
         tab2 = kept([P, T], U32, "tab2")
         tab3 = kept([P, T], U32, "tab3")
-        w2_raw = [kept([P, PACK, H], F32, "w2_raw%d" % a) for a in range(PASSES)]
+        w2_first = kept([P, PACK, H], F32, "w2_first")
+        w2_second = [kept([P, PACK, HALF], F32, "w2_second%d" % u) for u in range(2)]
         w1 = kept([P, PASSES, 2 * H], U8, "w1")
         w3 = kept([P, PASSES, H], U32, "w3")
         gain_sb = kept([P, PACK], F32, "gain_sb")
         d_sb = kept([P, S2 // P], F32, "d_sb")
         ident = kept([P, P], F32, "ident")
 
-        for plane in (tab3_plane, tab_plane, tab2_plane, w1_plane, w3_plane):
+        nc.gpsimd.memset(tab_plane[:, 0, :].bitcast(I32), 0)
+        nc.vector.memset(tab_plane[:, 1, :].bitcast(I32), 0)
+        for plane in (tab2_plane, tab3_plane, w1_plane, w3_plane):
             zero(nc.vector, plane)
 
-        def load_w2(a):
-            nc.sync.dma_start(out=w2_raw[a][:], in_=w2[512 * a : 512 * (a + 1), :].rearrange("(p i) c -> p i c", i=PACK))
+        def load_w2(dst, a, cols):
+            nc.sync.dma_start(out=dst, in_=w2[512 * a : 512 * (a + 1), cols].rearrange("(p i) c -> p i c", i=PACK))
 
         nc.sync.dma_start(out=idx1[:], in_=offs)
-        nc.sync.dma_start(out=idx2[:], in_=offs2)
-        nc.sync.dma_start(out=idx3[:], in_=offs3)
         load_words(tab[0], tab_words[0])
         load_scales(nc.sync, tab_plane, tab_scales, 0)
+        load_w2(w2_first[:], 0, slice(0, H))
+        nc.sync.dma_start(out=idx3[:], in_=offs3)
+        load_scales(nc.sync, tab3_plane, tab3_scales, ROW_V3)
         load_words(tab[1], tab_words[1])
         nc.sync.dma_start(out=w1[:].bitcast(I32), in_=w1_words.rearrange("a p c -> p a c").bitcast(I32))
         load_scales(nc.sync, w1_plane, w1_scales, 0)
-        load_w2(0)
+        for u in range(2):
+            load_w2(w2_second[u][:], 1, slice(HALF * u, HALF * (u + 1)))
+        nc.sync.dma_start(out=idx2[:], in_=offs2)
         load_scales(nc.sync, w3_plane, w3_scales, ROW_W3)
-        load_w2(1)
         nc.sync.dma_start(out=w3[:].bitcast(I32), in_=w3_words.rearrange("a p c i -> p a (c i)").bitcast(I32))
         load_words(tab2, tab2_words[0])
         load_words(tab3, tab3_words[0])
         make_identity(nc, ident[:])
-        load_scales(nc.gpsimd, tab3_plane, tab3_scales, ROW_V3)
         load_scales(nc.gpsimd, tab2_plane, tab2_scales, ROW_V2)
         nc.gpsimd.dma_start(out=gain_sb[:], in_=gain.rearrange("(p t) -> p t", t=PACK))
         with nc.allow_non_contiguous_dma(reason="one value of d for each partition and tile of candidates"):
@@ -108,10 +112,10 @@ def tile_list_hiker_date_scores_kernel(tc, tab_words, tab_scales, tab2_words, ta
         def gather(dst, window, idx):
             nc.vector.tensor_copy(out=dst, in_=window.indirect(idx))
 
-        def round_w2(copy, a, u):
+        def round_w2(copy, raw, a, u):
             copy(
                 out=w2_bf[a][u][:].rearrange("p (c e) i -> p c i e", e=4),
-                in_=w2_raw[a][:, :, HALF * u : HALF * (u + 1)].rearrange("p i (c e) -> p c i e", e=4),
+                in_=raw.rearrange("p i (c e) -> p c i e", e=4),
             )
 
         def quantize(codes, scales, grouped):
@@ -121,18 +125,21 @@ def tile_list_hiker_date_scores_kernel(tc, tab_words, tab_scales, tab2_words, ta
             cols = slice(HALF * u, HALF * (u + 1))
             quantize(w2_codes[a][:, cols], w2_sc[a][:, cols], w2_bf[a][u])
 
-        gather(v_sc[0][:], tab_plane[:, 0, :], idx1[:])
-        gather(v[0][:], tab[0][:], idx1[:])
-        gather(v_sc[1][:], tab_plane[:, 1, :], idx1[:])
-        gather(v[1][:], tab[1][:], idx1[:])
-        v3_sc = kept([P, S2], U8, "v3_sc", tag="tab1")
-        gather(v3_sc[:], tab3_plane[:, 0, :], idx3[:])
         for a in range(PASSES):
-            for u in range(2):
-                round_w2(nc.vector.tensor_copy, a, u)
-            for u in range(2):
-                quantize_w2(a, u)
-        v2_sc = kept([P, S2], U8, "v2_sc", tag="w2_raw1")
+            gather(v_sc[a][:], tab_plane[:, a, :], idx1[:])
+        gather(v[0][:], tab[0][:], idx1[:])
+        v3_sc = kept([P, S2], U8, "v3_sc")
+        gather(v3_sc[:], tab3_plane[:, 0, :], idx3[:])
+        for u in range(2):
+            round_w2(nc.scalar.copy, w2_first[:, :, HALF * u : HALF * (u + 1)], 0, u)
+        for u in range(2):
+            gather(v[1][:, HALF * u : HALF * (u + 1)], tab[1][:], idx1[:, 16 * u : 16 * (u + 1)])
+        for u in range(2):
+            quantize_w2(0, u)
+        for u in range(2):
+            round_w2(nc.vector.tensor_copy, w2_second[u][:], 1, u)
+            quantize_w2(1, u)
+        v2_sc = kept([P, S2], U8, "v2_sc")
         gather(v2_sc[:], tab2_plane[:, 0, :], idx2[:])
 
         weights = {
@@ -156,11 +163,12 @@ def tile_list_hiker_date_scores_kernel(tc, tab_words, tab_scales, tab2_words, ta
 
         def leave(kind, jt):
             vals[kind, jt] = work.tile([P, PACK, P], F32, name=kind)
-            src = banks[kind, jt][:].rearrange("p (m t) -> p t m", t=PACK)
+            src = banks[kind, jt][:].rearrange("p (m t) -> p m t", t=PACK)
+            dst = vals[kind, jt][:].rearrange("p t m -> p m t")
             if kind == "plain":
-                nc.scalar.copy(out=vals[kind, jt][:], in_=src)
+                nc.scalar.copy(out=dst, in_=src)
             else:
-                nc.scalar.activation(out=vals[kind, jt][:], in_=src, func=ACT.Tanh if kind == "taste" else ACT.Sin)
+                nc.scalar.activation(out=dst, in_=src, func=ACT.Tanh if kind == "taste" else ACT.Sin)
 
         def product(jt):
             vals["prod", jt] = work.tile([P, PACK, P], F32, name="prod")
@@ -223,19 +231,13 @@ def tile_list_hiker_date_scores_kernel(tc, tab_words, tab_scales, tab2_words, ta
             first_pass("pace", jt, 1)
             leave("pace", jt)
             whole("plain", jt)
+        for jt in range(4):
+            product(jt)
+            turn(jt)
+            if jt % 2:
+                quantize(h_codes[jt // 2][:], h_sc[jt // 2][:], h_bf[jt // 2])
         gather(v2[:], tab2[:], idx2[:])
-        product(0)
-        product(1)
-        turn(0)
-        product(2)
-        turn(1)
         gather(v3[:], tab3[:], idx3[:])
-        quantize(h_codes[0][:], h_sc[0][:], h_bf[0])
-        product(3)
-        turn(2)
-        partners(0)
-        trails(0)
-        turn(3)
-        quantize(h_codes[1][:], h_sc[1][:], h_bf[1])
-        partners(1)
-        trails(1)
+        for u in range(2):
+            partners(u)
+            trails(u)

@@ -40,10 +40,10 @@ def tile_list_hiker_date_scores_kernel(tc, tab_words, tab_scales, tab2_words, ta
             engine.memset(plane[:].rearrange("p a t -> p (a t)").bitcast(I32), 0)
 
         def load_scales(engine, plane, scales, row):
-            for q in range(4):
+            for r in range(4):
                 engine.dma_start(
-                    out=plane[32 * q + row : 32 * q + row + 4].bitcast(I32),
-                    in_=scales[:, 4 * q : 4 * q + 4, :].rearrange("a r t -> r a t").bitcast(I32),
+                    out=plane[row + r : P : 32].bitcast(I32),
+                    in_=scales[:, r:16:4, :].rearrange("a q t -> q a t").bitcast(I32),
                 )
 
         def load_words(tile, words):
@@ -163,8 +163,8 @@ def tile_list_hiker_date_scores_kernel(tc, tab_words, tab_scales, tab2_words, ta
 
         def leave(kind, jt):
             vals[kind, jt] = work.tile([P, PACK, P], F32, name=kind)
-            src = banks[kind, jt][:].rearrange("p (m t) -> p m t", t=PACK)
-            dst = vals[kind, jt][:].rearrange("p t m -> p m t")
+            src = banks[kind, jt][:].rearrange("p (g e t) -> p g t e", t=PACK, e=4)
+            dst = vals[kind, jt][:].rearrange("p t (g e) -> p g t e", e=4)
             if kind == "plain":
                 nc.scalar.copy(out=dst, in_=src)
             else:

from contextlib import ExitStack

import concourse.mybir as mybir
from concourse.masks import make_identity

K, T, S, H, S2 = 1024, 2048, 512, 512, 512
FLOPS = 2 * (3 * K * H * S + 2 * H * S2 * S)

F32 = mybir.dt.float32
BF16 = mybir.dt.bfloat16
I32 = mybir.dt.int32
U32 = mybir.dt.uint32
U16 = mybir.dt.uint16
U8 = mybir.dt.uint8
FP8X4 = mybir.dt.float8_e4m3fn_x4
FP4X4 = mybir.dt.float4_e2m1fn_x4
ACT = mybir.ActivationFunctionType
ALU = mybir.AluOpType

P = 128
PACK = 4
PASSES = K // (P * PACK)
HALF = 256
ROW_V2, ROW_V3, ROW_W3 = 4, 8, 12


def tile_list_hiker_date_scores_kernel(tc, tab_words, tab_scales, tab2_words, tab2_scales, tab3_words,
                                                 tab3_scales, offs, offs2, offs3, w1_words, w1_scales, w2,
                                                 w3_words, w3_scales, gain, d, out):
    nc = tc.nc
    with ExitStack() as ctx:
        keep = ctx.enter_context(tc.tile_pool(name="keep", bufs=1))
        work = ctx.enter_context(tc.tile_pool(name="work", bufs=4))
        psum = ctx.enter_context(tc.psum_pool(name="psum", bufs=1))

        def kept(shape, dtype, name, tag=None):
            return keep.tile(shape, dtype, name=name, tag=tag or name, align_bytes=64)

        def zero(engine, plane):
            engine.memset(plane[:].rearrange("p a t -> p (a t)").bitcast(I32), 0)

        def load_scales(engine, plane, scales, row):
            for r in range(4):
                engine.dma_start(
                    out=plane[row + r : P : 32].bitcast(I32),
                    in_=scales[:, r:16:4, :].rearrange("a q t -> q a t").bitcast(I32),
                )

        def load_words(tile, words):
            nc.sync.dma_start(out=tile[:].bitcast(I32), in_=words.rearrange("p t i -> p (t i)").bitcast(I32))

        idx1 = kept([P, S // 16], U16, "idx1")
        idx2 = kept([P, S2 // 16], U16, "idx2")
        idx3 = kept([P, S2 // 16], U16, "idx3")
        tab_plane = kept([P, PASSES, T], U8, "tab_plane")
        tab2_plane = kept([P, 1, T], U8, "tab2_plane")
        tab3_plane = kept([P, 1, T], U8, "tab3_plane")
        w1_plane = kept([P, PASSES, H], U8, "w1_plane")
        w3_plane = kept([P, PASSES, H], U8, "w3_plane")
        tab = [kept([P, T], U32, "tab%d" % a) for a in range(PASSES)]
        tab2 = kept([P, T], U32, "tab2")
        tab3 = kept([P, T], U32, "tab3")
        w2_first = kept([P, PACK, H], F32, "w2_first")
        w2_second = [kept([P, PACK, HALF], F32, "w2_second%d" % u) for u in range(2)]
        w1 = kept([P, PASSES, 2 * H], U8, "w1")
        w3 = kept([P, PASSES, H], U32, "w3")
        gain_sb = kept([P, PACK], F32, "gain_sb")
        d_sb = kept([P, S2 // P], F32, "d_sb")
        ident = kept([P, P], F32, "ident")

        nc.gpsimd.memset(tab_plane[:, 0, :].bitcast(I32), 0)
        nc.vector.memset(tab_plane[:, 1, :].bitcast(I32), 0)
        for plane in (tab2_plane, tab3_plane, w1_plane, w3_plane):
            zero(nc.vector, plane)

        def load_w2(dst, a, cols):
            nc.sync.dma_start(out=dst, in_=w2[512 * a : 512 * (a + 1), cols].rearrange("(p i) c -> p i c", i=PACK))

        nc.sync.dma_start(out=idx1[:], in_=offs)
        load_words(tab[0], tab_words[0])
        load_scales(nc.sync, tab_plane, tab_scales, 0)
        load_w2(w2_first[:], 0, slice(0, H))
        nc.sync.dma_start(out=idx3[:], in_=offs3)
        load_scales(nc.sync, tab3_plane, tab3_scales, ROW_V3)
        load_words(tab[1], tab_words[1])
        nc.sync.dma_start(out=w1[:].bitcast(I32), in_=w1_words.rearrange("a p c -> p a c").bitcast(I32))
        load_scales(nc.sync, w1_plane, w1_scales, 0)
        for u in range(2):
            load_w2(w2_second[u][:], 1, slice(HALF * u, HALF * (u + 1)))
        nc.sync.dma_start(out=idx2[:], in_=offs2)
        load_scales(nc.sync, w3_plane, w3_scales, ROW_W3)
        nc.sync.dma_start(out=w3[:].bitcast(I32), in_=w3_words.rearrange("a p c i -> p a (c i)").bitcast(I32))
        load_words(tab2, tab2_words[0])
        load_words(tab3, tab3_words[0])
        make_identity(nc, ident[:])
        load_scales(nc.gpsimd, tab2_plane, tab2_scales, ROW_V2)
        nc.gpsimd.dma_start(out=gain_sb[:], in_=gain.rearrange("(p t) -> p t", t=PACK))
        with nc.allow_non_contiguous_dma(reason="one value of d for each partition and tile of candidates"):
            nc.gpsimd.dma_start(out=d_sb[:], in_=d.rearrange("(c p) -> p c", p=P))

        v = [kept([P, S], U32, "v%d" % a) for a in range(PASSES)]
        v_sc = [kept([P, S], U8, "v_sc%d" % a) for a in range(PASSES)]
        v2 = kept([P, S2], U32, "v2")
        v3 = kept([P, S2], U32, "v3")
        w2_bf = [[kept([P, HALF, PACK], BF16, "w2_bf%d%d" % (a, u)) for u in range(2)] for a in range(PASSES)]
        w2_codes = [kept([P, H], U32, "w2_codes%d" % a) for a in range(PASSES)]
        w2_sc = [kept([P, H], U8, "w2_sc%d" % a) for a in range(PASSES)]
        h_bf = [kept([P, HALF, PACK], BF16, "h_bf%d" % u) for u in range(2)]
        h_codes = [kept([P, HALF], U32, "h_codes%d" % u) for u in range(2)]
        h_sc = [kept([P, HALF], U8, "h_sc%d" % u) for u in range(2)]

        def gather(dst, window, idx):
            nc.vector.tensor_copy(out=dst, in_=window.indirect(idx))

        def round_w2(copy, raw, a, u):
            copy(
                out=w2_bf[a][u][:].rearrange("p (c e) i -> p c i e", e=4),
                in_=raw.rearrange("p i (c e) -> p c i e", e=4),
            )

        def quantize(codes, scales, grouped):
            nc.vector.quantize_mx(out=codes.bitcast(FP8X4), scales=scales, in_=grouped[:].rearrange("p c i -> p (c i)"))

        def quantize_w2(a, u):
            cols = slice(HALF * u, HALF * (u + 1))
            quantize(w2_codes[a][:, cols], w2_sc[a][:, cols], w2_bf[a][u])

        for a in range(PASSES):
            gather(v_sc[a][:], tab_plane[:, a, :], idx1[:])
        gather(v[0][:], tab[0][:], idx1[:])
        v3_sc = kept([P, S2], U8, "v3_sc")
        gather(v3_sc[:], tab3_plane[:, 0, :], idx3[:])
        for u in range(2):
            round_w2(nc.scalar.copy, w2_first[:, :, HALF * u : HALF * (u + 1)], 0, u)
        for u in range(2):
            gather(v[1][:, HALF * u : HALF * (u + 1)], tab[1][:], idx1[:, 16 * u : 16 * (u + 1)])
        for u in range(2):
            quantize_w2(0, u)
        for u in range(2):
            round_w2(nc.vector.tensor_copy, w2_second[u][:], 1, u)
            quantize_w2(1, u)
        v2_sc = kept([P, S2], U8, "v2_sc")
        gather(v2_sc[:], tab2_plane[:, 0, :], idx2[:])

        weights = {
            "taste": lambda a: (w1[:, a, :].bitcast(FP4X4), w1_plane[:, a, :]),
            "pace": lambda a: (w2_codes[a][:].bitcast(FP8X4), w2_sc[a][:]),
            "plain": lambda a: (w3[:, a, :].bitcast(FP8X4), w3_plane[ROW_W3:, a, :]),
        }
        banks = {}
        vals = {}

        def new_bank():
            return psum.tile([P, 512], F32, name="bank", tag="bank", bufs=6)

        def first_pass(kind, jt, a):
            if a == 0:
                banks[kind, jt] = new_bank()
            cols = slice(P * jt, P * (jt + 1))
            codes, scales = weights[kind](a)
            nc.tensor.matmul_mx(out=banks[kind, jt][:], lhsT=v[a][:, cols].bitcast(FP8X4), lhsT_scale=v_sc[a][:, cols],
                                rhs=codes, rhs_scale=scales, start=(a == 0), stop=(a == PASSES - 1))

        def leave(kind, jt):
            vals[kind, jt] = work.tile([P, PACK, P], F32, name=kind)
            src = banks[kind, jt][:].rearrange("p (g e t) -> p g t e", t=PACK, e=4)
            dst = vals[kind, jt][:].rearrange("p t (g e) -> p g t e", e=4)
            if kind == "plain":
                nc.scalar.copy(out=dst, in_=src)
            else:
                nc.scalar.activation(out=dst, in_=src, func=ACT.Tanh if kind == "taste" else ACT.Sin)

        def product(jt):
            vals["prod", jt] = work.tile([P, PACK, P], F32, name="prod")
            nc.vector.tensor_tensor(out=vals["prod", jt][:], in0=vals["taste", jt][:], in1=vals["pace", jt][:], op=ALU.mult)

        def turn(jt):
            turned = psum.tile([P, PACK, P], F32, name="turned", tag="turned", bufs=2)
            for t in range(PACK):
                nc.tensor.matmul(out=turned[:, t, :], lhsT=vals["plain", jt][:, t, :], rhs=ident[:],
                                 is_transpose=True, start=True, stop=False)
                nc.tensor.matmul(out=turned[:, t, :], lhsT=vals["prod", jt][:, t, :], rhs=ident[:],
                                 is_transpose=True, start=False, stop=True)
            u, c = divmod(jt, 2)
            nc.vector.tensor_tensor(
                out=h_bf[u][:, P * c : P * (c + 1), :],
                in0=turned[:].rearrange("p t j -> p j t"),
                in1=gain_sb[:].unsqueeze(1).to_broadcast([P, P, PACK]),
                op=ALU.mult,
            )

        def scores(codes, scales, row, u, pair):
            bank = new_bank()
            for c in range(2):
                cols = slice(P * (2 * pair + c), P * (2 * pair + c + 1))
                nc.tensor.matmul_mx(out=bank[:, HALF * c : HALF * (c + 1)], lhsT=codes[:, cols].bitcast(FP8X4),
                                    lhsT_scale=scales[row:, cols], rhs=h_codes[u][:].bitcast(FP8X4),
                                    rhs_scale=h_sc[u][:], start=True, stop=True)
            return bank

        def partners(u):
            for pair in range(2):
                bank = scores(v2, v2_sc, ROW_V2, u, pair)
                for c in range(2):
                    mt = 2 * pair + c
                    vals["e2", u, mt] = work.tile([P, HALF], F32, name="e2", bufs=8)
                    nc.scalar.activation(out=vals["e2", u, mt][:], in_=bank[:, HALF * c : HALF * (c + 1)],
                                         func=ACT.Identity, bias=d_sb[:, mt : mt + 1])

        def trails(u):
            for pair in range(2):
                bank = scores(v3, v3_sc, ROW_V3, u, pair)
                for c in range(2):
                    mt = 2 * pair + c
                    result = work.tile([P, HALF], F32, name="result", bufs=8)
                    nc.vector.scalar_tensor_tensor(out=result[:], in0=bank[:, HALF * c : HALF * (c + 1)],
                                                   scalar=d_sb[:, mt : mt + 1], in1=vals["e2", u, mt][:],
                                                   op0=ALU.add, op1=ALU.min)
                    nc.sync.dma_start(out=out[P * mt : P * (mt + 1), HALF * u : HALF * (u + 1)], in_=result[:])

        def whole(kind, jt):
            first_pass(kind, jt, 0)
            first_pass(kind, jt, 1)
            leave(kind, jt)

        for jt in range(4):
            whole("taste", jt)
        for jt in range(4):
            first_pass("pace", jt, 0)
        for jt in range(4):
            first_pass("pace", jt, 1)
            leave("pace", jt)
            whole("plain", jt)
        for jt in range(4):
            product(jt)
            turn(jt)
            if jt % 2:
                quantize(h_codes[jt // 2][:], h_sc[jt // 2][:], h_bf[jt // 2])
        gather(v2[:], tab2[:], idx2[:])
        gather(v3[:], tab3[:], idx3[:])
        for u in range(2):
            partners(u)
            trails(u)
